import numpy as np
import ml_dtypes


def mxq(x, axis, fmt="e4m3"):
    dtype, down = {"e4m3": (ml_dtypes.float8_e4m3fn, 7), "e5m2": (ml_dtypes.float8_e5m2, 14)}[fmt]
    v = np.moveaxis(np.asarray(x, np.float32).astype(ml_dtypes.bfloat16).astype(np.float64), axis, -1)
    blocks = v.reshape(v.shape[:-1] + (-1, 32))
    amax = np.abs(blocks).max(-1, keepdims=True)
    byte = np.maximum(np.where(amax > 0, np.frexp(amax)[1] - 1 + 127, 0) - down, 1)
    scale = np.exp2(byte - 127.0)
    codes = (blocks / scale).astype(np.float32).astype(dtype).astype(np.float64)
    return np.moveaxis((codes * scale).reshape(v.shape), -1, axis)


WIDE = False


def mx_kscale(k):
    if not WIDE:
        return np.ones(k)
    levels = np.array([10, -10, 5, -5, 0])
    if k % 512:
        return np.exp2(np.random.permutation(np.resize(levels, k // 32))).repeat(32)
    a = np.empty((k // 512, 16))
    for p in range(k // 512):
        a[p, :8] = np.random.permutation(np.resize(levels, 8))
        for g in range(8):
            far = levels[np.abs(levels - a[p, g]) >= 10]
            a[p, g + 8] = far[np.random.randint(len(far))]
    return np.exp2(a.ravel()).repeat(32)


def f64(x):
    return np.asarray(x).astype(np.float64)


def striped(idx):
    return np.tile(idx.reshape(-1, 16).T, (8, 1)).astype(np.uint16)


def unstriped(offs):
    return offs[:16].T.reshape(-1).astype(np.int64)


E2M1 = np.array([0.0, 0.5, 1.0, 1.5, 2.0, 3.0, 4.0, 6.0, -0.0, -0.5, -1.0, -1.5, -2.0, -3.0, -4.0, -6.0])


def pack_weight(w, fmt):
    k, n = w.shape
    w = f64(np.asarray(w, np.float32).astype(ml_dtypes.bfloat16)).reshape(k // 32, 32, n)
    amax = np.abs(w).max(1)
    if fmt == "e4m3":
        byte = np.frexp(amax)[1] - 1 + 127 - 7
    else:
        mant, ex = np.frexp(amax / 6.0)
        byte = np.where(mant > 0.5, ex, ex - 1) + 127
    byte = np.clip(np.where(amax > 0, byte, 1), 1, 254)
    scaled = (w * np.exp2(127.0 - byte)[:, None, :]).reshape(k, n).astype(np.float32)
    by_word = np.ascontiguousarray(scaled.reshape(k // 512, 128, 4, n).transpose(0, 1, 3, 2))
    if fmt == "e4m3":
        words = by_word.astype(ml_dtypes.float8_e4m3fn).view(np.uint8)
    else:
        c = by_word.astype(ml_dtypes.float4_e2m1fn).view(np.uint8) & 0xF
        words = (c[..., 0::2] | (c[..., 1::2] << 4)).reshape(k // 512, 128, 2 * n)
    return np.ascontiguousarray(words), np.ascontiguousarray(byte.astype(np.uint8).reshape(k // 512, 16, n))


def unpack_weight(words, scales, fmt):
    g, _, n = scales.shape
    words = np.ascontiguousarray(words).reshape(g, 128, n, -1)
    if fmt == "e4m3":
        vals = words.view(ml_dtypes.float8_e4m3fn).astype(np.float64)
    else:
        nib = np.empty((g, 128, n, 4), np.uint8)
        nib[..., 0::2] = words & 0xF
        nib[..., 1::2] = words >> 4
        vals = E2M1[nib]
    vals = vals * np.repeat(np.exp2(scales.astype(np.float64) - 127.0), 8, axis=1)[..., None]
    return vals.transpose(0, 1, 3, 2).reshape(g * 512, n)


def gelu(v):
    return 0.5 * v * (1.0 + np.tanh(np.sqrt(2.0 / np.pi) * (v + 0.044715 * v**3)))


def striped8(idx):
    return np.concatenate([v.reshape(-1, 16).T for v in idx]).astype(np.uint16)


def unstriped8(offs):
    return np.stack([offs[16 * g:16 * g + 16].T.reshape(-1) for g in range(8)]).astype(np.int64)


def heads(h, wgt, idx8):
    r = np.arange(h.shape[0])
    return wgt[r // 4 % 128] * h[r[:, None], idx8[r % 512 // 64]]


def put_heads(h, wgs, idx8, t2):
    r = np.arange(h.shape[0])
    page = np.zeros((h.shape[0], t2))
    page[r[:, None], idx8[r % 512 // 64]] = wgs[r // 4 % 128] * h
    return page


K, T, S, P, T2, R, H, N = 512, 4096, 1024, 512, 1024, 1024, 1024, 1024

def setup_inputs():
    n = np.random.standard_normal
    s, u1, u = mx_kscale(K)[:, None], mx_kscale(R)[:, None], mx_kscale(H)[:, None]
    d = {}
    d["tab_words"], d["tab_scales"] = pack_weight(n((K, T)) * s, "e4m3")
    d["offs"] = striped(np.random.permutation(T)[:S])
    d["offs2"] = striped8(np.stack([np.random.permutation(S)[:P] for _ in range(8)]))
    d["offs3"] = striped8(np.stack([np.random.permutation(T2)[:P] for _ in range(8)]))
    d["w1"] = (1.6 * n((K, R)) / K ** 0.5 / s).astype(np.float32)
    d["fgain"] = (np.exp(0.3 * n(R)) * u1[:, 0]).astype(np.float32)
    d["w2_words"], d["w2_scales"] = pack_weight(n((R, H)) / R ** 0.5 / u1, "e2m1")
    d["w3"] = (n((K, H)) / K ** 0.5 / s * u.T).astype(np.float32)
    d["wgt"] = np.repeat(np.random.uniform(0.5, 2.0, (8, P)), 16, axis=0).astype(np.float32)
    d["plan"] = (0.8 * n((H, P)) * u).astype(np.float32)
    d["w4_words"], d["w4_scales"] = pack_weight(0.8 * n((H, N)) / H ** 0.5 / u, "e4m3")
    d["rgain"] = (0.6 * np.exp(0.3 * n(H)) / u[:, 0]).astype(np.float32)
    d["wgo"] = np.repeat(np.random.uniform(0.5, 2.0, (8, P)), 16, axis=0).astype(np.float32)
    return d

def reference(tab_words, tab_scales, offs, offs2, offs3, w1, fgain, w2_words, w2_scales, w3, wgt, plan, w4_words, w4_scales, rgain, wgo):
    v = unpack_weight(tab_words, tab_scales, "e4m3")[:, unstriped(offs)]
    w2 = unpack_weight(w2_words, w2_scales, "e2m1")
    w4 = unpack_weight(w4_words, w4_scales, "e4m3")
    f = np.tanh(mxq(f64(w1), 0, "e4m3").T @ v) * f64(fgain)[:, None]
    proj = w2.T @ mxq(f, 0, "e4m3")
    h = proj * (mxq(f64(w3), 0, "e4m3").T @ v)
    x = heads(h, f64(wgt), unstriped8(offs2))
    z = x + f64(plan)
    y = np.square((w4.T @ mxq(z, 0, "e4m3")) - z * f64(rgain)[:, None])
    return put_heads(y, f64(wgo), unstriped8(offs3), T2)

@@ -1,0 +1,287 @@
+from contextlib import ExitStack
+
+import concourse.mybir as mybir
+from concourse.masks import make_identity
+
+K, T, S, M, T2, R, H, N = 512, 4096, 1024, 512, 1024, 1024, 1024, 1024
+FLOPS = 2 * (K * R * S + R * H * S + K * H * S + H * N * M)
+
+F32 = mybir.dt.float32
+BF16 = mybir.dt.bfloat16
+I32 = mybir.dt.int32
+U32 = mybir.dt.uint32
+U16 = mybir.dt.uint16
+U8 = mybir.dt.uint8
+FP8X4 = mybir.dt.float8_e4m3fn_x4
+FP4X4 = mybir.dt.float4_e2m1fn_x4
+MULT = mybir.AluOpType.mult
+ADD = mybir.AluOpType.add
+ACT = mybir.ActivationFunctionType
+
+P = 128
+PACK = 4
+PASS = P * PACK
+BANK = 512
+HALF = M // 2
+
+
+def tile_list_denture_depth_features_kernel(
+    tc, tab_words, tab_scales, offs, offs2, offs3, w1, fgain, w2_words, w2_scales, w3, wgt, plan,
+    w4_words, w4_scales, rgain, wgo, out,
+):
+    nc = tc.nc
+    with ExitStack() as ctx:
+        lists = ctx.enter_context(tc.tile_pool(name="lists", bufs=1))
+        keep = ctx.enter_context(tc.tile_pool(name="keep", bufs=1))
+        ring = ctx.enter_context(tc.tile_pool(name="ring", bufs=1))
+        arena = ctx.enter_context(tc.tile_pool(name="arena", bufs=1))
+        psum = ctx.enter_context(tc.psum_pool(name="psum", bufs=1))
+
+        def held(shape, dtype, name):
+            return keep.tile(shape, dtype, name=name, align_bytes=64)
+
+        def turn(shape, dtype, name, tag, bufs):
+            return ring.tile(shape, dtype, name=name, tag=tag, bufs=bufs, align_bytes=64)
+
+        def placed(shape, dtype, name, unit):
+            return arena.tile(shape, dtype, name=name, align_bytes=64, offset=2048 * unit)
+
+        def bank(name, tag):
+            return psum.tile([P, BANK], F32, name=name, tag=tag, bufs={"f": 3, "lin": 2, "proj": 3}[tag])
+
+        def load_scales(queue, plane, scales):
+            for r in range(4):
+                queue.dma_start(
+                    out=plane[r:P:32, :, :].bitcast(I32),
+                    in_=scales[:, r:16:4, :].rearrange("a q c -> q a c").bitcast(I32),
+                )
+
+        idx = lists.tile([P, S // 16], U16, name="idx")
+        idx2 = lists.tile([P, M // 16], U16, name="idx2")
+        idx3 = lists.tile([P, M // 16], U16, name="idx3")
+        tab_s = held([P, T], U8, "tab_s")
+        w2s_raw = held([P, 2, H], U8, "w2s_raw")
+        w4s = held([P, 2, N], U8, "w4s")
+        nc.vector.memset(w2s_raw[:].bitcast(I32), 0)
+        nc.vector.memset(tab_s[:].bitcast(I32), 0)
+        nc.vector.memset(w4s[:].bitcast(I32), 0)
+
+        def load_weight(w, b, name, unit):
+            raw = placed([P, PACK, PASS], F32, name, unit)
+            nc.sync.dma_start(out=raw[:], in_=w[:, PASS * b:PASS * (b + 1)].rearrange("(p j) c -> p j c", j=PACK))
+            return raw
+
+        tab_w = turn([P, T], I32, "tab_w", "wide", 1)
+        tab_hbm = tab_words[0].rearrange("p t i -> p (t i)").bitcast(I32)
+        nc.sync.dma_start(out=tab_w[:, :T // 2], in_=tab_hbm[:, :T // 2])
+        load_scales(nc.sync, w2s_raw, w2_scales)
+        nc.sync.dma_start(out=tab_w[:, T // 2:], in_=tab_hbm[:, T // 2:])
+        nc.sync.dma_start(idx[:], offs)
+        for r in range(4):
+            nc.sync.dma_start(out=tab_s[r:P:32, :].bitcast(I32), in_=tab_scales[0, r:16:4, :].bitcast(I32))
+        w1_raw = [load_weight(w1, 0, "w1_raw0", 0)]
+        fg = held([P, 2, PACK], F32, "fg")
+        nc.sync.dma_start(out=fg[:], in_=fgain.rearrange("(b p t) -> p b t", b=2, t=PACK))
+        w1_raw.append(load_weight(w1, 1, "w1_raw1", 4))
+        w2w_raw = held([P, 2, 2 * H], U8, "w2w_raw")
+        nc.sync.dma_start(out=w2w_raw[:].bitcast(I32), in_=w2_words.rearrange("a p c -> p a c").bitcast(I32))
+        w3_raw = [load_weight(w3, b, "w3_raw%d" % b, 8 + 4 * b) for b in range(2)]
+        nc.sync.dma_start(idx2[:], offs2)
+        wgt_t = held([P, M], F32, "wgt_t")
+        nc.sync.dma_start(out=wgt_t[:], in_=wgt)
+        plan_t = [held([P, PACK, M], F32, "plan%d" % b) for b in range(2)]
+        for b in range(2):
+            nc.sync.dma_start(out=plan_t[b][:], in_=plan[PASS * b:PASS * (b + 1), :].rearrange("(p i) m -> p i m", i=PACK))
+        rg = held([P, 2, PACK], F32, "rg")
+        nc.sync.dma_start(out=rg[:], in_=rgain.rearrange("(b p t) -> p b t", b=2, t=PACK))
+        load_scales(nc.sync, w4s, w4_scales)
+        w4w = held([P, 2, N], I32, "w4w")
+        nc.sync.dma_start(out=w4w[:], in_=w4_words.rearrange("a p c i -> p a (c i)").bitcast(I32))
+        nc.sync.dma_start(idx3[:], offs3)
+        wgo_t = held([P, M], F32, "wgo_t")
+        nc.sync.dma_start(out=wgo_t[:], in_=wgo)
+
+        ident = held([P, P], F32, "ident")
+        make_identity(nc, ident[:])
+        pages = [held([P, T2], F32, "page%d" % k) for k in range(8)]
+        for page in pages[:5]:
+            nc.gpsimd.memset(page[:], 0.0)
+        for page in pages[5:]:
+            nc.vector.memset(page[:], 0.0)
+
+        w2s = held([P, 2, H], U8, "w2s")
+        nc.vector.tensor_copy(
+            out=w2s[:].rearrange("p a (b t q) -> p (a b) t q", b=2, t=PACK),
+            in_=w2s_raw[:].rearrange("p a (b q t) -> p (a b) t q", b=2, t=PACK),
+        )
+
+        def round_weight(copy, raw, name):
+            rounded = turn([P, PASS * PACK], BF16, name, "bf", 3)
+            copy(
+                out=rounded[:].rearrange("p (t q j) -> p q t j", t=PACK, j=PACK),
+                in_=raw[:].rearrange("p j (q t) -> p q t j", t=PACK),
+            )
+            return rounded
+
+        def quantise(rounded, width, name):
+            words = held([P, width], U32, name + "_w")
+            scales = held([P, width], U8, name + "_s")
+            nc.vector.quantize_mx(out=words[:].bitcast(FP8X4), scales=scales[:], in_=rounded)
+            return words, scales
+
+        def mx(acc, lhs, lcols, rhs, rcols, start, stop):
+            nc.tensor.matmul_mx(
+                out=acc, lhsT=lhs[0][:, lcols].bitcast(FP8X4), lhsT_scale=lhs[1][:, lcols],
+                rhs=rhs[0][:, rcols].bitcast(FP8X4), rhs_scale=rhs[1][:, rcols], start=start, stop=stop,
+            )
+
+        w1q = [quantise(round_weight(nc.scalar.copy, w1_raw[0], "w1_bf0")[:], PASS, "w1q0")]
+        v_w = [held([P, BANK], U32, "v_w%d" % c) for c in range(2)]
+        v_s = [held([P, BANK], U8, "v_s%d" % c) for c in range(2)]
+        for c in range(2):
+            cut = idx[:, 32 * c:32 * (c + 1)]
+            nc.vector.tensor_copy(v_w[c][:], tab_w[:].bitcast(U32).indirect(cut))
+            nc.vector.tensor_copy(v_s[c][:], tab_s[:].indirect(cut))
+        w1q.append(quantise(round_weight(nc.vector.tensor_copy, w1_raw[1], "w1_bf1")[:], PASS, "w1q1"))
+        w2w = held([P, 2, 2 * H], U8, "w2w")
+        nc.vector.tensor_copy(
+            out=w2w[:].bitcast(U16).rearrange("p a (b t q) -> p (a b) t q", b=2, t=PACK),
+            in_=w2w_raw[:].bitcast(U16).rearrange("p a (b q t) -> p (a b) t q", b=2, t=PACK),
+        )
+
+        fq = {}
+        w3q = []
+        for b in range(2):
+            for c in range(2):
+                f_bf = turn([P, BANK * PACK], BF16, "f_bf%d%d" % (b, c), "bf", 3)
+                for u in range(2):
+                    th = turn([P, 2 * P * PACK], F32, "th%d%d%d" % (b, c, u), "four", 4)
+                    for s in range(2):
+                        acc = bank("a%d%d%d%d" % (b, c, u, s), "f")
+                        j0 = (2 * u + s) * P
+                        for t in range(PACK):
+                            mx(acc[:, P * t:P * (t + 1)], w1q[b], slice(P * t, P * (t + 1)), (v_w[c], v_s[c]), slice(j0, j0 + P), True, True)
+                        nc.scalar.activation(
+                            out=th[:, BANK * s:BANK * (s + 1)].rearrange("p (j t) -> p j t", t=PACK),
+                            in_=acc[:].rearrange("p (t j) -> p j t", t=PACK), func=ACT.Tanh,
+                        )
+                    nc.vector.tensor_tensor(
+                        out=f_bf[:, 1024 * u:1024 * (u + 1)].rearrange("p (j t) -> p j t", t=PACK),
+                        in0=th[:].rearrange("p (j t) -> p j t", t=PACK),
+                        in1=fg[:, b, :].unsqueeze(1).to_broadcast([P, 2 * P, PACK]), op=MULT,
+                    )
+                fq[b, c] = quantise(f_bf[:], BANK, "fq%d%d" % (b, c))
+            w3q.append(quantise(round_weight(nc.scalar.copy, w3_raw[b], "w3_bf%d" % b)[:], PASS, "w3q%d" % b))
+
+        h = [held([P, S], F32, "h%d" % k) for k in range(8)]
+        x = [held([P, HALF], F32, "x%d" % k) for k in range(2)]
+        z = turn([P, 2, 2, PACK, HALF], F32, "z", "wide", 1)
+        zq = {}
+        turned = {}
+
+        def make_h(k):
+            b, i = divmod(k, PACK)
+            cols = slice(P * i, P * (i + 1))
+            for c in range(2):
+                lin_ps = bank("lin%d%d" % (k, c), "lin")
+                mx(lin_ps[:], w3q[b], cols, (v_w[c], v_s[c]), slice(0, BANK), True, True)
+                lin = turn([P, BANK], F32, "lin_sb%d%d" % (k, c), "lin", 4)
+                nc.scalar.copy(out=lin[:], in_=lin_ps[:])
+                proj = bank("proj%d%d" % (k, c), "proj")
+                for a in range(2):
+                    nc.tensor.matmul_mx(
+                        out=proj[:], lhsT=w2w[:, a, 2 * P * k:2 * P * (k + 1)].bitcast(FP4X4),
+                        lhsT_scale=w2s[:, a, P * k:P * (k + 1)],
+                        rhs=fq[a, c][0][:].bitcast(FP8X4), rhs_scale=fq[a, c][1][:], start=(a == 0), stop=(a == 1),
+                    )
+                nc.vector.tensor_tensor(out=h[k][:, BANK * c:BANK * (c + 1)], in0=proj[:], in1=lin[:], op=MULT)
+
+        def gather(k, e):
+            nc.vector.tensor_tensor(
+                x[k % 2][:], h[k][:].indirect(idx2[:, 16 * e:16 * (e + 1)]), wgt_t[:, HALF * e:HALF * (e + 1)], MULT,
+            )
+
+        def add_plan(k, e):
+            b, i = divmod(k, PACK)
+            nc.vector.tensor_tensor(out=z[:, e, b, i, :], in0=x[k % 2][:], in1=plan_t[b][:, i, HALF * e:HALF * (e + 1)], op=ADD)
+            if i == PACK - 1:
+                finish_z(b, e)
+
+        def finish_z(b, e):
+            late = (b, e) == (0, 1)
+            z_bf = placed([P, HALF * PACK], BF16, "z_late", 0) if late else turn([P, HALF * PACK], BF16, "z_bf%d%d" % (e, b), "bf", 3)
+            nc.scalar.copy(out=z_bf[:].rearrange("p (m i) -> p m i", i=PACK), in_=z[:, e, b, :, :].rearrange("p i m -> p m i"))
+            zq[b, e] = quantise(z_bf[:], HALF, "zq%d%d" % (e, b))
+            zr = placed([P, PACK, HALF], F32, "zr_late", 2) if late else turn([P, PACK, HALF], F32, "zr%d%d" % (e, b), "four", 4)
+            for i in range(PACK):
+                nc.scalar.activation(out=zr[:, i, :], in_=z[:, e, b, i, :], func=ACT.Copy, scale=rg[:, b, i:i + 1])
+            for s in range(2):
+                turned[e, b, s, 0] = placed([P, PASS], F32, "zr_t%d%d%d" % (e, b, s), 8 * e + 4 * b + 2 + s)
+                ps = bank("zrT%d%d%d" % (e, b, s), "f")
+                for i in range(PACK):
+                    nc.tensor.transpose(ps[:, P * i:P * (i + 1)], zr[:, i, P * s:P * (s + 1)], ident[:])
+                nc.scalar.copy(out=turned[e, b, s, 0][:], in_=ps[:])
+
+        def last_product(b, e):
+            for s in range(2):
+                ps = bank("pT%d%d%d" % (e, b, s), "lin")
+                cols = slice(P * s, P * (s + 1))
+                for a in range(2):
+                    nc.tensor.matmul_mx(
+                        out=ps[:], lhsT=zq[a, e][0][:, cols].bitcast(FP8X4), lhsT_scale=zq[a, e][1][:, cols],
+                        rhs=w4w[:, a, PASS * b:PASS * (b + 1)].bitcast(FP8X4), rhs_scale=w4s[:, a, PASS * b:PASS * (b + 1)],
+                        start=(a == 0), stop=(a == 1),
+                    )
+                turned[e, b, s, 1] = placed([P, PASS], F32, "prod_t%d%d%d" % (e, b, s), 8 * e + 4 * b + s)
+                nc.scalar.activation(
+                    out=turned[e, b, s, 1][:].rearrange("m (i p) -> m i p", i=PACK),
+                    in_=ps[:].rearrange("m (p i) -> m i p", i=PACK), func=ACT.Copy, scale=-1.0,
+                )
+
+        def squares(b, e, pair):
+            ps = bank("d%d%d%d" % (e, b, pair), "proj")
+            for u in range(2):
+                i = 2 * pair + u
+                for s in range(2):
+                    dst = ps[:, HALF * u + P * s:HALF * u + P * (s + 1)]
+                    for w in range(2):
+                        nc.tensor.matmul(
+                            dst, turned[e, b, s, w][:, P * i:P * (i + 1)], ident[:],
+                            start=(w == 0), stop=(w == 1), is_transpose=True,
+                        )
+            y = turn([P, BANK], F32, "y%d%d%d" % (e, b, pair), "y", 4)
+            nc.scalar.activation(out=y[:], in_=ps[:], func=ACT.Square)
+            return y
+
+        def results(b, e):
+            last_product(b, e)
+            return [squares(b, e, pair) for pair in range(2)]
+
+        def place(b, e, ys):
+            rows = out.rearrange("(b p i) t -> b i p t", b=2, i=PACK)
+            for i in range(PACK):
+                page = pages[PACK * b + i]
+                nc.vector.tensor_tensor(
+                    page[:].indirect(idx3[:, 16 * e:16 * (e + 1)]), ys[i // 2][:, HALF * (i % 2):HALF * (i % 2 + 1)],
+                    wgo_t[:, HALF * e:HALF * (e + 1)], MULT,
+                )
+                if e == 1:
+                    nc.sync.dma_start(out=rows[b, i], in_=page[:])
+
+        for k in range(8):
+            make_h(k)
+            if k > 0:
+                add_plan(k - 1, 0)
+            gather(k, 0)
+        gather_order = list(range(8))
+        add_plan(7, 0)
+        first = results(0, 0)
+        for k in gather_order:
+            gather(k, 1)
+            if k > 0:
+                add_plan(k - 1, 1)
+        add_plan(7, 1)
+        place(0, 0, first)
+        place(1, 0, results(1, 0))
+        for b in range(2):
+            place(b, 1, results(b, 1))

@@ -60,7 +60,7 @@ def tile_list_denture_depth_features_kernel(
         idx2 = lists.tile([P, M // 16], U16, name="idx2")
         idx3 = lists.tile([P, M // 16], U16, name="idx3")
         tab_s = held([P, T], U8, "tab_s")
-        w2s_raw = held([P, 2, H], U8, "w2s_raw")
+        w2s_raw = turn([P, 2, H], U8, "w2s_raw", "y", 4)
         w4s = held([P, 2, N], U8, "w4s")
         nc.vector.memset(w2s_raw[:].bitcast(I32), 0)
         nc.vector.memset(tab_s[:].bitcast(I32), 0)
@@ -71,6 +71,11 @@ def tile_list_denture_depth_features_kernel(
             nc.sync.dma_start(out=raw[:], in_=w[:, PASS * b:PASS * (b + 1)].rearrange("(p j) c -> p j c", j=PACK))
             return raw
 
+        def load_half(u):
+            raw = placed([P, PACK, HALF], F32, "w1_raw0%d" % u, 2 * u)
+            nc.sync.dma_start(out=raw[:], in_=w1[:, HALF * u:HALF * (u + 1)].rearrange("(p j) c -> p j c", j=PACK))
+            return raw
+
         tab_w = turn([P, T], I32, "tab_w", "wide", 1)
         tab_hbm = tab_words[0].rearrange("p t i -> p (t i)").bitcast(I32)
         nc.sync.dma_start(out=tab_w[:, :T // 2], in_=tab_hbm[:, :T // 2])
@@ -79,7 +84,7 @@ def tile_list_denture_depth_features_kernel(
         nc.sync.dma_start(idx[:], offs)
         for r in range(4):
             nc.sync.dma_start(out=tab_s[r:P:32, :].bitcast(I32), in_=tab_scales[0, r:16:4, :].bitcast(I32))
-        w1_raw = [load_weight(w1, 0, "w1_raw0", 0)]
+        w1_raw = [[load_half(u) for u in range(2)]]
         fg = held([P, 2, PACK], F32, "fg")
         nc.sync.dma_start(out=fg[:], in_=fgain.rearrange("(b p t) -> p b t", b=2, t=PACK))
         w1_raw.append(load_weight(w1, 1, "w1_raw1", 4))
@@ -116,7 +121,7 @@ def tile_list_denture_depth_features_kernel(
         )
 
         def round_weight(copy, raw, name):
-            rounded = turn([P, PASS * PACK], BF16, name, "bf", 3)
+            rounded = turn([P, PASS * PACK], BF16, name, "bf", 4)
             copy(
                 out=rounded[:].rearrange("p (t q j) -> p q t j", t=PACK, j=PACK),
                 in_=raw[:].rearrange("p j (q t) -> p q t j", t=PACK),
@@ -135,7 +140,13 @@ def tile_list_denture_depth_features_kernel(
                 rhs=rhs[0][:, rcols].bitcast(FP8X4), rhs_scale=rhs[1][:, rcols], start=start, stop=stop,
             )
 
-        w1q = [quantise(round_weight(nc.scalar.copy, w1_raw[0], "w1_bf0")[:], PASS, "w1q0")]
+        w1_bf = turn([P, PASS * PACK], BF16, "w1_bf0", "bf", 4)
+        for u in range(2):
+            nc.scalar.copy(
+                out=w1_bf[:].rearrange("p (t q j) -> p q t j", t=PACK, j=PACK)[:, 64 * u:64 * (u + 1), :, :],
+                in_=w1_raw[0][u][:].rearrange("p j (q t) -> p q t j", t=PACK),
+            )
+        w1q = [quantise(w1_bf[:], PASS, "w1q0")]
         v_w = [held([P, BANK], U32, "v_w%d" % c) for c in range(2)]
         v_s = [held([P, BANK], U8, "v_s%d" % c) for c in range(2)]
         for c in range(2):
@@ -151,30 +162,43 @@ def tile_list_denture_depth_features_kernel(
 
         fq = {}
         w3q = []
+        waiting = []
+
+        def apply_gain(f_bf, th, b, lo, hi):
+            nc.vector.tensor_tensor(
+                out=f_bf[:, lo:hi].rearrange("p (j t) -> p j t", t=PACK),
+                in0=th[:, lo:hi].rearrange("p (j t) -> p j t", t=PACK),
+                in1=fg[:, b, :].unsqueeze(1).to_broadcast([P, (hi - lo) // PACK, PACK]), op=MULT,
+            )
+
         for b in range(2):
             for c in range(2):
-                f_bf = turn([P, BANK * PACK], BF16, "f_bf%d%d" % (b, c), "bf", 3)
+                f_bf = turn([P, BANK * PACK], BF16, "f_bf%d%d" % (b, c), "bf", 4)
+                th = turn([P, BANK * PACK], F32, "th%d%d" % (b, c), "eight", 2)
                 for u in range(2):
-                    th = turn([P, 2 * P * PACK], F32, "th%d%d%d" % (b, c, u), "four", 4)
                     for s in range(2):
                         acc = bank("a%d%d%d%d" % (b, c, u, s), "f")
                         j0 = (2 * u + s) * P
                         for t in range(PACK):
                             mx(acc[:, P * t:P * (t + 1)], w1q[b], slice(P * t, P * (t + 1)), (v_w[c], v_s[c]), slice(j0, j0 + P), True, True)
                         nc.scalar.activation(
-                            out=th[:, BANK * s:BANK * (s + 1)].rearrange("p (j t) -> p j t", t=PACK),
+                            out=th[:, PACK * j0:PACK * (j0 + P)].rearrange("p (j t) -> p j t", t=PACK),
                             in_=acc[:].rearrange("p (t j) -> p j t", t=PACK), func=ACT.Tanh,
                         )
-                    nc.vector.tensor_tensor(
-                        out=f_bf[:, 1024 * u:1024 * (u + 1)].rearrange("p (j t) -> p j t", t=PACK),
-                        in0=th[:].rearrange("p (j t) -> p j t", t=PACK),
-                        in1=fg[:, b, :].unsqueeze(1).to_broadcast([P, 2 * P, PACK]), op=MULT,
-                    )
-                fq[b, c] = quantise(f_bf[:], BANK, "fq%d%d" % (b, c))
+                    if (b, c) == (0, 0):
+                        apply_gain(f_bf, th, b, 1024 * u, 1024 * (u + 1))
+                if (b, c) != (0, 0):
+                    apply_gain(f_bf, th, b, 0, 2048)
+                if waiting:
+                    key, done = waiting.pop()
+                    fq[key] = quantise(done[:], BANK, "fq%d%d" % key)
+                waiting.append(((b, c), f_bf))
             w3q.append(quantise(round_weight(nc.scalar.copy, w3_raw[b], "w3_bf%d" % b)[:], PASS, "w3q%d" % b))
+        key, done = waiting.pop()
+        fq[key] = quantise(done[:], BANK, "fq%d%d" % key)
 
         h = [held([P, S], F32, "h%d" % k) for k in range(8)]
-        x = [held([P, HALF], F32, "x%d" % k) for k in range(2)]
+        x = {0: held([P, 2, HALF], F32, "x0")}
         z = turn([P, 2, 2, PACK, HALF], F32, "z", "wide", 1)
         zq = {}
         turned = {}
@@ -185,7 +209,10 @@ def tile_list_denture_depth_features_kernel(
             for c in range(2):
                 lin_ps = bank("lin%d%d" % (k, c), "lin")
                 mx(lin_ps[:], w3q[b], cols, (v_w[c], v_s[c]), slice(0, BANK), True, True)
-                lin = turn([P, BANK], F32, "lin_sb%d%d" % (k, c), "lin", 4)
+                if (k, c) == (7, 0):
+                    lin = placed([P, BANK], F32, "lin_last", 12)
+                else:
+                    lin = turn([P, BANK], F32, "lin_sb%d%d" % (k, c), "lin", 3)
                 nc.scalar.copy(out=lin[:], in_=lin_ps[:])
                 proj = bank("proj%d%d" % (k, c), "proj")
                 for a in range(2):
@@ -198,21 +225,22 @@ def tile_list_denture_depth_features_kernel(
 
         def gather(k, e):
             nc.vector.tensor_tensor(
-                x[k % 2][:], h[k][:].indirect(idx2[:, 16 * e:16 * (e + 1)]), wgt_t[:, HALF * e:HALF * (e + 1)], MULT,
+                x[e][:, k % (2 + 2 * e), :], h[k][:].indirect(idx2[:, 16 * e:16 * (e + 1)]), wgt_t[:, HALF * e:HALF * (e + 1)], MULT,
             )
 
-        def add_plan(k, e):
+        def add_plan(k, e, count=1):
             b, i = divmod(k, PACK)
-            nc.vector.tensor_tensor(out=z[:, e, b, i, :], in0=x[k % 2][:], in1=plan_t[b][:, i, HALF * e:HALF * (e + 1)], op=ADD)
+            rows = slice(i - count + 1, i + 1)
+            nc.vector.tensor_tensor(out=z[:, e, b, rows, :], in0=x[e][:, rows, :] if e else x[0][:, k % 2:k % 2 + 1, :], in1=plan_t[b][:, rows, HALF * e:HALF * (e + 1)], op=ADD)
             if i == PACK - 1:
                 finish_z(b, e)
 
         def finish_z(b, e):
             late = (b, e) == (0, 1)
-            z_bf = placed([P, HALF * PACK], BF16, "z_late", 0) if late else turn([P, HALF * PACK], BF16, "z_bf%d%d" % (e, b), "bf", 3)
+            z_bf = placed([P, HALF * PACK], BF16, "z_late", 0) if late else turn([P, HALF * PACK], BF16, "z_bf%d%d" % (e, b), "bf", 4)
             nc.scalar.copy(out=z_bf[:].rearrange("p (m i) -> p m i", i=PACK), in_=z[:, e, b, :, :].rearrange("p i m -> p m i"))
             zq[b, e] = quantise(z_bf[:], HALF, "zq%d%d" % (e, b))
-            zr = placed([P, PACK, HALF], F32, "zr_late", 2) if late else turn([P, PACK, HALF], F32, "zr%d%d" % (e, b), "four", 4)
+            zr = placed([P, PACK, HALF], F32, "zr_late", 2) if late else turn([P, PACK, HALF], F32, "zr%d%d" % (e, b), "eight", 2)
             for i in range(PACK):
                 nc.scalar.activation(out=zr[:, i, :], in_=z[:, e, b, i, :], func=ACT.Copy, scale=rg[:, b, i:i + 1])
             for s in range(2):
@@ -273,14 +301,15 @@ def tile_list_denture_depth_features_kernel(
             if k > 0:
                 add_plan(k - 1, 0)
             gather(k, 0)
-        gather_order = list(range(8))
+        x[1] = placed([P, PACK, HALF], F32, "x1", 12)
+        gather(0, 1)
         add_plan(7, 0)
         first = results(0, 0)
-        for k in gather_order:
+        for k in range(1, 8):
             gather(k, 1)
-            if k > 0:
-                add_plan(k - 1, 1)
-        add_plan(7, 1)
+            if k % 2 == 0:
+                add_plan(k - 1, 1, 2)
+        add_plan(7, 1, 2)
         place(0, 0, first)
         place(1, 0, results(1, 0))
         for b in range(2):

@@ -109,9 +109,7 @@ def tile_list_denture_depth_features_kernel(
         ident = held([P, P], F32, "ident")
         make_identity(nc, ident[:])
         pages = [held([P, T2], F32, "page%d" % k) for k in range(8)]
-        for page in pages[:5]:
-            nc.gpsimd.memset(page[:], 0.0)
-        for page in pages[5:]:
+        for page in pages:
             nc.vector.memset(page[:], 0.0)
 
         w2s = held([P, 2, H], U8, "w2s")
@@ -140,6 +138,12 @@ def tile_list_denture_depth_features_kernel(
                 rhs=rhs[0][:, rcols].bitcast(FP8X4), rhs_scale=rhs[1][:, rcols], start=start, stop=stop,
             )
 
+        v_w = [held([P, BANK], U32, "v_w%d" % c) for c in range(2)]
+        v_s = [held([P, BANK], U8, "v_s%d" % c) for c in range(2)]
+        for c in range(2):
+            cut = idx[:, 32 * c:32 * (c + 1)]
+            nc.vector.tensor_copy(v_w[c][:], tab_w[:].bitcast(U32).indirect(cut))
+            nc.vector.tensor_copy(v_s[c][:], tab_s[:].indirect(cut))
         w1_bf = turn([P, PASS * PACK], BF16, "w1_bf0", "bf", 4)
         for u in range(2):
             nc.scalar.copy(
@@ -147,12 +151,6 @@ def tile_list_denture_depth_features_kernel(
                 in_=w1_raw[0][u][:].rearrange("p j (q t) -> p q t j", t=PACK),
             )
         w1q = [quantise(w1_bf[:], PASS, "w1q0")]
-        v_w = [held([P, BANK], U32, "v_w%d" % c) for c in range(2)]
-        v_s = [held([P, BANK], U8, "v_s%d" % c) for c in range(2)]
-        for c in range(2):
-            cut = idx[:, 32 * c:32 * (c + 1)]
-            nc.vector.tensor_copy(v_w[c][:], tab_w[:].bitcast(U32).indirect(cut))
-            nc.vector.tensor_copy(v_s[c][:], tab_s[:].indirect(cut))
         w1q.append(quantise(round_weight(nc.vector.tensor_copy, w1_raw[1], "w1_bf1")[:], PASS, "w1q1"))
         w2w = held([P, 2, 2 * H], U8, "w2w")
         nc.vector.tensor_copy(
@@ -185,13 +183,13 @@ def tile_list_denture_depth_features_kernel(
                             out=th[:, PACK * j0:PACK * (j0 + P)].rearrange("p (j t) -> p j t", t=PACK),
                             in_=acc[:].rearrange("p (t j) -> p j t", t=PACK), func=ACT.Tanh,
                         )
-                    if (b, c) == (0, 0):
+                    if b == c:
                         apply_gain(f_bf, th, b, 1024 * u, 1024 * (u + 1))
-                if (b, c) != (0, 0):
-                    apply_gain(f_bf, th, b, 0, 2048)
-                if waiting:
-                    key, done = waiting.pop()
-                    fq[key] = quantise(done[:], BANK, "fq%d%d" % key)
+                    elif u == 1:
+                        apply_gain(f_bf, th, b, 0, 2048)
+                    if waiting and (b == c or u == 1):
+                        key, done = waiting.pop()
+                        fq[key] = quantise(done[:], BANK, "fq%d%d" % key)
                 waiting.append(((b, c), f_bf))
             w3q.append(quantise(round_weight(nc.scalar.copy, w3_raw[b], "w3_bf%d" % b)[:], PASS, "w3q%d" % b))
         key, done = waiting.pop()
@@ -212,7 +210,7 @@ def tile_list_denture_depth_features_kernel(
                 if (k, c) == (7, 0):
                     lin = placed([P, BANK], F32, "lin_last", 12)
                 else:
-                    lin = turn([P, BANK], F32, "lin_sb%d%d" % (k, c), "lin", 3)
+                    lin = turn([P, BANK], F32, "lin_sb%d%d" % (k, c), "lin", 4)
                 nc.scalar.copy(out=lin[:], in_=lin_ps[:])
                 proj = bank("proj%d%d" % (k, c), "proj")
                 for a in range(2):

from contextlib import ExitStack

import concourse.mybir as mybir
from concourse.masks import make_identity

K, T, S, M, T2, R, H, N = 512, 4096, 1024, 512, 1024, 1024, 1024, 1024
FLOPS = 2 * (K * R * S + R * H * S + K * H * S + H * N * M)

F32 = mybir.dt.float32
BF16 = mybir.dt.bfloat16
I32 = mybir.dt.int32
U32 = mybir.dt.uint32
U16 = mybir.dt.uint16
U8 = mybir.dt.uint8
FP8X4 = mybir.dt.float8_e4m3fn_x4
FP4X4 = mybir.dt.float4_e2m1fn_x4
MULT = mybir.AluOpType.mult
ADD = mybir.AluOpType.add
ACT = mybir.ActivationFunctionType

P = 128
PACK = 4
PASS = P * PACK
BANK = 512
HALF = M // 2


def tile_list_denture_depth_features_kernel(
    tc, tab_words, tab_scales, offs, offs2, offs3, w1, fgain, w2_words, w2_scales, w3, wgt, plan,
    w4_words, w4_scales, rgain, wgo, out,
):
    nc = tc.nc
    with ExitStack() as ctx:
        lists = ctx.enter_context(tc.tile_pool(name="lists", bufs=1))
        keep = ctx.enter_context(tc.tile_pool(name="keep", bufs=1))
        ring = ctx.enter_context(tc.tile_pool(name="ring", bufs=1))
        arena = ctx.enter_context(tc.tile_pool(name="arena", bufs=1))
        psum = ctx.enter_context(tc.psum_pool(name="psum", bufs=1))

        def held(shape, dtype, name):
            return keep.tile(shape, dtype, name=name, align_bytes=64)

        def turn(shape, dtype, name, tag, bufs):
            return ring.tile(shape, dtype, name=name, tag=tag, bufs=bufs, align_bytes=64)

        def placed(shape, dtype, name, unit):
            return arena.tile(shape, dtype, name=name, align_bytes=64, offset=2048 * unit)

        def bank(name, tag):
            return psum.tile([P, BANK], F32, name=name, tag=tag, bufs={"f": 3, "lin": 2, "proj": 3}[tag])

        def load_scales(queue, plane, scales):
            for r in range(4):
                queue.dma_start(
                    out=plane[r:P:32, :, :].bitcast(I32),
                    in_=scales[:, r:16:4, :].rearrange("a q c -> q a c").bitcast(I32),
                )

        idx = lists.tile([P, S // 16], U16, name="idx")
        idx2 = lists.tile([P, M // 16], U16, name="idx2")
        idx3 = lists.tile([P, M // 16], U16, name="idx3")
        tab_s = held([P, T], U8, "tab_s")
        w2s_raw = turn([P, 2, H], U8, "w2s_raw", "y", 4)
        w4s = held([P, 2, N], U8, "w4s")
        nc.vector.memset(w2s_raw[:].bitcast(I32), 0)
        nc.vector.memset(tab_s[:].bitcast(I32), 0)
        nc.vector.memset(w4s[:].bitcast(I32), 0)

        def load_weight(w, b, name, unit):
            raw = placed([P, PACK, PASS], F32, name, unit)
            nc.sync.dma_start(out=raw[:], in_=w[:, PASS * b:PASS * (b + 1)].rearrange("(p j) c -> p j c", j=PACK))
            return raw

        def load_half(u):
            raw = placed([P, PACK, HALF], F32, "w1_raw0%d" % u, 2 * u)
            nc.sync.dma_start(out=raw[:], in_=w1[:, HALF * u:HALF * (u + 1)].rearrange("(p j) c -> p j c", j=PACK))
            return raw

        tab_w = turn([P, T], I32, "tab_w", "wide", 1)
        tab_hbm = tab_words[0].rearrange("p t i -> p (t i)").bitcast(I32)
        nc.sync.dma_start(out=tab_w[:, :T // 2], in_=tab_hbm[:, :T // 2])
        load_scales(nc.sync, w2s_raw, w2_scales)
        nc.sync.dma_start(out=tab_w[:, T // 2:], in_=tab_hbm[:, T // 2:])
        nc.sync.dma_start(idx[:], offs)
        for r in range(4):
            nc.sync.dma_start(out=tab_s[r:P:32, :].bitcast(I32), in_=tab_scales[0, r:16:4, :].bitcast(I32))
        w1_raw = [[load_half(u) for u in range(2)]]
        fg = held([P, 2, PACK], F32, "fg")
        nc.sync.dma_start(out=fg[:], in_=fgain.rearrange("(b p t) -> p b t", b=2, t=PACK))
        w1_raw.append(load_weight(w1, 1, "w1_raw1", 4))
        w2w_raw = held([P, 2, 2 * H], U8, "w2w_raw")
        nc.sync.dma_start(out=w2w_raw[:].bitcast(I32), in_=w2_words.rearrange("a p c -> p a c").bitcast(I32))
        w3_raw = [load_weight(w3, b, "w3_raw%d" % b, 8 + 4 * b) for b in range(2)]
        nc.sync.dma_start(idx2[:], offs2)
        wgt_t = held([P, M], F32, "wgt_t")
        nc.sync.dma_start(out=wgt_t[:], in_=wgt)
        plan_t = [held([P, PACK, M], F32, "plan%d" % b) for b in range(2)]
        for b in range(2):
            nc.sync.dma_start(out=plan_t[b][:], in_=plan[PASS * b:PASS * (b + 1), :].rearrange("(p i) m -> p i m", i=PACK))
        rg = held([P, 2, PACK], F32, "rg")
        nc.sync.dma_start(out=rg[:], in_=rgain.rearrange("(b p t) -> p b t", b=2, t=PACK))
        load_scales(nc.sync, w4s, w4_scales)
        w4w = held([P, 2, N], I32, "w4w")
        nc.sync.dma_start(out=w4w[:], in_=w4_words.rearrange("a p c i -> p a (c i)").bitcast(I32))
        nc.sync.dma_start(idx3[:], offs3)
        wgo_t = held([P, M], F32, "wgo_t")
        nc.sync.dma_start(out=wgo_t[:], in_=wgo)

        ident = held([P, P], F32, "ident")
        make_identity(nc, ident[:])
        pages = [held([P, T2], F32, "page%d" % k) for k in range(8)]
        for page in pages:
            nc.vector.memset(page[:], 0.0)

        w2s = held([P, 2, H], U8, "w2s")
        nc.vector.tensor_copy(
            out=w2s[:].rearrange("p a (b t q) -> p (a b) t q", b=2, t=PACK),
            in_=w2s_raw[:].rearrange("p a (b q t) -> p (a b) t q", b=2, t=PACK),
        )

        def round_weight(copy, raw, name):
            rounded = turn([P, PASS * PACK], BF16, name, "bf", 4)
            copy(
                out=rounded[:].rearrange("p (t q j) -> p q t j", t=PACK, j=PACK),
                in_=raw[:].rearrange("p j (q t) -> p q t j", t=PACK),
            )
            return rounded

        def quantise(rounded, width, name):
            words = held([P, width], U32, name + "_w")
            scales = held([P, width], U8, name + "_s")
            nc.vector.quantize_mx(out=words[:].bitcast(FP8X4), scales=scales[:], in_=rounded)
            return words, scales

        def mx(acc, lhs, lcols, rhs, rcols, start, stop):
            nc.tensor.matmul_mx(
                out=acc, lhsT=lhs[0][:, lcols].bitcast(FP8X4), lhsT_scale=lhs[1][:, lcols],
                rhs=rhs[0][:, rcols].bitcast(FP8X4), rhs_scale=rhs[1][:, rcols], start=start, stop=stop,
            )

        v_w = [held([P, BANK], U32, "v_w%d" % c) for c in range(2)]
        v_s = [held([P, BANK], U8, "v_s%d" % c) for c in range(2)]
        for c in range(2):
            cut = idx[:, 32 * c:32 * (c + 1)]
            nc.vector.tensor_copy(v_w[c][:], tab_w[:].bitcast(U32).indirect(cut))
            nc.vector.tensor_copy(v_s[c][:], tab_s[:].indirect(cut))
        w1_bf = turn([P, PASS * PACK], BF16, "w1_bf0", "bf", 4)
        for u in range(2):
            nc.scalar.copy(
                out=w1_bf[:].rearrange("p (t q j) -> p q t j", t=PACK, j=PACK)[:, 64 * u:64 * (u + 1), :, :],
                in_=w1_raw[0][u][:].rearrange("p j (q t) -> p q t j", t=PACK),
            )
        w1q = [quantise(w1_bf[:], PASS, "w1q0")]
        w1q.append(quantise(round_weight(nc.vector.tensor_copy, w1_raw[1], "w1_bf1")[:], PASS, "w1q1"))
        w2w = held([P, 2, 2 * H], U8, "w2w")
        nc.vector.tensor_copy(
            out=w2w[:].bitcast(U16).rearrange("p a (b t q) -> p (a b) t q", b=2, t=PACK),
            in_=w2w_raw[:].bitcast(U16).rearrange("p a (b q t) -> p (a b) t q", b=2, t=PACK),
        )

        fq = {}
        w3q = []
        waiting = []

        def apply_gain(f_bf, th, b, lo, hi):
            nc.vector.tensor_tensor(
                out=f_bf[:, lo:hi].rearrange("p (j t) -> p j t", t=PACK),
                in0=th[:, lo:hi].rearrange("p (j t) -> p j t", t=PACK),
                in1=fg[:, b, :].unsqueeze(1).to_broadcast([P, (hi - lo) // PACK, PACK]), op=MULT,
            )

        for b in range(2):
            for c in range(2):
                f_bf = turn([P, BANK * PACK], BF16, "f_bf%d%d" % (b, c), "bf", 4)
                th = turn([P, BANK * PACK], F32, "th%d%d" % (b, c), "eight", 2)
                for u in range(2):
                    for s in range(2):
                        acc = bank("a%d%d%d%d" % (b, c, u, s), "f")
                        j0 = (2 * u + s) * P
                        for t in range(PACK):
                            mx(acc[:, P * t:P * (t + 1)], w1q[b], slice(P * t, P * (t + 1)), (v_w[c], v_s[c]), slice(j0, j0 + P), True, True)
                        nc.scalar.activation(
                            out=th[:, PACK * j0:PACK * (j0 + P)].rearrange("p (j t) -> p j t", t=PACK),
                            in_=acc[:].rearrange("p (t j) -> p j t", t=PACK), func=ACT.Tanh,
                        )
                    if b == c:
                        apply_gain(f_bf, th, b, 1024 * u, 1024 * (u + 1))
                    elif u == 1:
                        apply_gain(f_bf, th, b, 0, 2048)
                    if waiting and (b == c or u == 1):
                        key, done = waiting.pop()
                        fq[key] = quantise(done[:], BANK, "fq%d%d" % key)
                waiting.append(((b, c), f_bf))
            w3q.append(quantise(round_weight(nc.scalar.copy, w3_raw[b], "w3_bf%d" % b)[:], PASS, "w3q%d" % b))
        key, done = waiting.pop()
        fq[key] = quantise(done[:], BANK, "fq%d%d" % key)

        h = [held([P, S], F32, "h%d" % k) for k in range(8)]
        x = {0: held([P, 2, HALF], F32, "x0")}
        z = turn([P, 2, 2, PACK, HALF], F32, "z", "wide", 1)
        zq = {}
        turned = {}

        def make_h(k):
            b, i = divmod(k, PACK)
            cols = slice(P * i, P * (i + 1))
            for c in range(2):
                lin_ps = bank("lin%d%d" % (k, c), "lin")
                mx(lin_ps[:], w3q[b], cols, (v_w[c], v_s[c]), slice(0, BANK), True, True)
                if (k, c) == (7, 0):
                    lin = placed([P, BANK], F32, "lin_last", 12)
                else:
                    lin = turn([P, BANK], F32, "lin_sb%d%d" % (k, c), "lin", 4)
                nc.scalar.copy(out=lin[:], in_=lin_ps[:])
                proj = bank("proj%d%d" % (k, c), "proj")
                for a in range(2):
                    nc.tensor.matmul_mx(
                        out=proj[:], lhsT=w2w[:, a, 2 * P * k:2 * P * (k + 1)].bitcast(FP4X4),
                        lhsT_scale=w2s[:, a, P * k:P * (k + 1)],
                        rhs=fq[a, c][0][:].bitcast(FP8X4), rhs_scale=fq[a, c][1][:], start=(a == 0), stop=(a == 1),
                    )
                nc.vector.tensor_tensor(out=h[k][:, BANK * c:BANK * (c + 1)], in0=proj[:], in1=lin[:], op=MULT)

        def gather(k, e):
            nc.vector.tensor_tensor(
                x[e][:, k % (2 + 2 * e), :], h[k][:].indirect(idx2[:, 16 * e:16 * (e + 1)]), wgt_t[:, HALF * e:HALF * (e + 1)], MULT,
            )

        def add_plan(k, e, count=1):
            b, i = divmod(k, PACK)
            rows = slice(i - count + 1, i + 1)
            nc.vector.tensor_tensor(out=z[:, e, b, rows, :], in0=x[e][:, rows, :] if e else x[0][:, k % 2:k % 2 + 1, :], in1=plan_t[b][:, rows, HALF * e:HALF * (e + 1)], op=ADD)
            if i == PACK - 1:
                finish_z(b, e)

        def finish_z(b, e):
            late = (b, e) == (0, 1)
            z_bf = placed([P, HALF * PACK], BF16, "z_late", 0) if late else turn([P, HALF * PACK], BF16, "z_bf%d%d" % (e, b), "bf", 4)
            nc.scalar.copy(out=z_bf[:].rearrange("p (m i) -> p m i", i=PACK), in_=z[:, e, b, :, :].rearrange("p i m -> p m i"))
            zq[b, e] = quantise(z_bf[:], HALF, "zq%d%d" % (e, b))
            zr = placed([P, PACK, HALF], F32, "zr_late", 2) if late else turn([P, PACK, HALF], F32, "zr%d%d" % (e, b), "eight", 2)
            for i in range(PACK):
                nc.scalar.activation(out=zr[:, i, :], in_=z[:, e, b, i, :], func=ACT.Copy, scale=rg[:, b, i:i + 1])
            for s in range(2):
                turned[e, b, s, 0] = placed([P, PASS], F32, "zr_t%d%d%d" % (e, b, s), 8 * e + 4 * b + 2 + s)
                ps = bank("zrT%d%d%d" % (e, b, s), "f")
                for i in range(PACK):
                    nc.tensor.transpose(ps[:, P * i:P * (i + 1)], zr[:, i, P * s:P * (s + 1)], ident[:])
                nc.scalar.copy(out=turned[e, b, s, 0][:], in_=ps[:])

        def last_product(b, e):
            for s in range(2):
                ps = bank("pT%d%d%d" % (e, b, s), "lin")
                cols = slice(P * s, P * (s + 1))
                for a in range(2):
                    nc.tensor.matmul_mx(
                        out=ps[:], lhsT=zq[a, e][0][:, cols].bitcast(FP8X4), lhsT_scale=zq[a, e][1][:, cols],
                        rhs=w4w[:, a, PASS * b:PASS * (b + 1)].bitcast(FP8X4), rhs_scale=w4s[:, a, PASS * b:PASS * (b + 1)],
                        start=(a == 0), stop=(a == 1),
                    )
                turned[e, b, s, 1] = placed([P, PASS], F32, "prod_t%d%d%d" % (e, b, s), 8 * e + 4 * b + s)
                nc.scalar.activation(
                    out=turned[e, b, s, 1][:].rearrange("m (i p) -> m i p", i=PACK),
                    in_=ps[:].rearrange("m (p i) -> m i p", i=PACK), func=ACT.Copy, scale=-1.0,
                )

        def squares(b, e, pair):
            ps = bank("d%d%d%d" % (e, b, pair), "proj")
            for u in range(2):
                i = 2 * pair + u
                for s in range(2):
                    dst = ps[:, HALF * u + P * s:HALF * u + P * (s + 1)]
                    for w in range(2):
                        nc.tensor.matmul(
                            dst, turned[e, b, s, w][:, P * i:P * (i + 1)], ident[:],
                            start=(w == 0), stop=(w == 1), is_transpose=True,
                        )
            y = turn([P, BANK], F32, "y%d%d%d" % (e, b, pair), "y", 4)
            nc.scalar.activation(out=y[:], in_=ps[:], func=ACT.Square)
            return y

        def results(b, e):
            last_product(b, e)
            return [squares(b, e, pair) for pair in range(2)]

        def place(b, e, ys):
            rows = out.rearrange("(b p i) t -> b i p t", b=2, i=PACK)
            for i in range(PACK):
                page = pages[PACK * b + i]
                nc.vector.tensor_tensor(
                    page[:].indirect(idx3[:, 16 * e:16 * (e + 1)]), ys[i // 2][:, HALF * (i % 2):HALF * (i % 2 + 1)],
                    wgo_t[:, HALF * e:HALF * (e + 1)], MULT,
                )
                if e == 1:
                    nc.sync.dma_start(out=rows[b, i], in_=page[:])

        for k in range(8):
            make_h(k)
            if k > 0:
                add_plan(k - 1, 0)
            gather(k, 0)
        x[1] = placed([P, PACK, HALF], F32, "x1", 12)
        gather(0, 1)
        add_plan(7, 0)
        first = results(0, 0)
        for k in range(1, 8):
            gather(k, 1)
            if k % 2 == 0:
                add_plan(k - 1, 1, 2)
        add_plan(7, 1, 2)
        place(0, 0, first)
        place(1, 0, results(1, 0))
        for b in range(2):
            place(b, 1, results(b, 1))
